import numpy as np
import ml_dtypes


def mxq(x, axis, fmt="e4m3"):
    dtype, down = {"e4m3": (ml_dtypes.float8_e4m3fn, 7), "e5m2": (ml_dtypes.float8_e5m2, 14)}[fmt]
    v = np.moveaxis(np.asarray(x, np.float32).astype(ml_dtypes.bfloat16).astype(np.float64), axis, -1)
    blocks = v.reshape(v.shape[:-1] + (-1, 32))
    amax = np.abs(blocks).max(-1, keepdims=True)
    byte = np.maximum(np.where(amax > 0, np.frexp(amax)[1] - 1 + 127, 0) - down, 1)
    scale = np.exp2(byte - 127.0)
    codes = (blocks / scale).astype(np.float32).astype(dtype).astype(np.float64)
    return np.moveaxis((codes * scale).reshape(v.shape), -1, axis)


WIDE = False


def mx_kscale(k):
    if not WIDE:
        return np.ones(k)
    levels = np.array([10, -10, 5, -5, 0])
    if k % 512:
        return np.exp2(np.random.permutation(np.resize(levels, k // 32))).repeat(32)
    a = np.empty((k // 512, 16))
    for p in range(k // 512):
        a[p, :8] = np.random.permutation(np.resize(levels, 8))
        for g in range(8):
            far = levels[np.abs(levels - a[p, g]) >= 10]
            a[p, g + 8] = far[np.random.randint(len(far))]
    return np.exp2(a.ravel()).repeat(32)


def f64(x):
    return np.asarray(x).astype(np.float64)


def striped(idx):
    return np.tile(np.asarray(idx).reshape(-1, 16).T, (8, 1)).astype(np.uint16)


def unstriped(offs):
    return offs[:16].T.reshape(-1).astype(np.int64)


E2M1 = np.array([0.0, 0.5, 1.0, 1.5, 2.0, 3.0, 4.0, 6.0, -0.0, -0.5, -1.0, -1.5, -2.0, -3.0, -4.0, -6.0])


def pack_weight(w, fmt):
    k, n = w.shape
    w = f64(np.asarray(w, np.float32).astype(ml_dtypes.bfloat16)).reshape(k // 32, 32, n)
    amax = np.abs(w).max(1)
    if fmt == "e4m3":
        byte = np.frexp(amax)[1] - 1 + 127 - 7
    else:
        mant, ex = np.frexp(amax / 6.0)
        byte = np.where(mant > 0.5, ex, ex - 1) + 127
    byte = np.clip(np.where(amax > 0, byte, 1), 1, 254)
    scaled = (w * np.exp2(127.0 - byte)[:, None, :]).reshape(k, n).astype(np.float32)
    by_word = np.ascontiguousarray(scaled.reshape(k // 512, 128, 4, n).transpose(0, 1, 3, 2))
    if fmt == "e4m3":
        words = by_word.astype(ml_dtypes.float8_e4m3fn).view(np.uint8)
    else:
        c = by_word.astype(ml_dtypes.float4_e2m1fn).view(np.uint8) & 0xF
        words = (c[..., 0::2] | (c[..., 1::2] << 4)).reshape(k // 512, 128, 2 * n)
    return np.ascontiguousarray(words), np.ascontiguousarray(byte.astype(np.uint8).reshape(k // 512, 16, n))


def unpack_weight(words, scales, fmt):
    g, _, n = scales.shape
    words = np.ascontiguousarray(words).reshape(g, 128, n, -1)
    if fmt == "e4m3":
        vals = words.view(ml_dtypes.float8_e4m3fn).astype(np.float64)
    else:
        nib = np.empty((g, 128, n, 4), np.uint8)
        nib[..., 0::2] = words & 0xF
        nib[..., 1::2] = words >> 4
        vals = E2M1[nib]
    vals = vals * np.repeat(np.exp2(scales.astype(np.float64) - 127.0), 8, axis=1)[..., None]
    return vals.transpose(0, 1, 3, 2).reshape(g * 512, n)


def bf(x):
    return np.asarray(x, np.float32).astype(ml_dtypes.bfloat16)


def planes(Y):
    r, m = Y.shape
    b = f64(bf(Y)).reshape(r // 32, 32, m)
    amax = np.abs(b).max(1)
    byte = np.clip(np.where(amax > 0, np.frexp(amax)[1] - 1 + 127 - 7, 1), 1, 254)
    codes = (b * np.exp2(127.0 - byte)[:, None, :]).reshape(r, m).astype(np.float32).astype(ml_dtypes.float8_e4m3fn).view(np.uint8)
    words = codes.reshape(r // 512, 128, 4, m).transpose(0, 1, 3, 2)
    return np.ascontiguousarray(words), np.ascontiguousarray(byte.astype(np.uint8).reshape(r // 512, 16, m))


K, T, J, B, L, N = 1024, 2048, 512, 128, 512, 512


def setup_inputs():
    n = np.random.standard_normal
    idx = np.random.permutation(T)[:J]
    fk = mx_kscale(K)
    fl = mx_kscale(L)
    wp = pack_weight(n((K, N)) * 1 / np.sqrt(K) * fk[:, None], "e2m1")
    xsp = pack_weight(n((L, J)) / fl[:, None], "e4m3")
    wsp = pack_weight(n((L, N)) * 1 / np.sqrt(L) * fl[:, None], "e2m1")
    return {
        "xt": (n((K, T)) / fk[:, None]).astype(np.float32),
        "w_words": wp[0],
        "w_scales": wp[1],
        "xs_words": xsp[0],
        "xs_scales": xsp[1],
        "ws_words": wsp[0],
        "ws_scales": wsp[1],
        "offs": striped(idx),
    }


def reference(xt, w_words, w_scales, xs_words, xs_scales, ws_words, ws_scales, offs):
    idx = unstriped(offs)
    wu = unpack_weight(w_words, w_scales, "e2m1")
    xsu = unpack_weight(xs_words, xs_scales, "e4m3")
    wsu = unpack_weight(ws_words, ws_scales, "e2m1")
    xtidxq = mxq(f64(xt)[:, idx], 0, "e4m3")
    z = wu.T @ xtidxq
    u = z.reshape(N, B, J // B).max(axis=2)
    ur = np.repeat(u, J // B, axis=1)
    q = wsu.T @ xsu
    y = z * np.exp(z - ur) + 0.5 * q
    words, scales = planes(y)
    return y, words, scales

@@ -1,0 +1,195 @@
+from contextlib import ExitStack
+
+import concourse.mybir as mybir
+
+K, T, J, N = 1024, 2048, 512, 512
+FLOPS = 2 * (K + 512) * N * J
+
+F32 = mybir.dt.float32
+BF16 = mybir.dt.bfloat16
+I32 = mybir.dt.int32
+U32 = mybir.dt.uint32
+U16 = mybir.dt.uint16
+U8 = mybir.dt.uint8
+FP8X4 = mybir.dt.float8_e4m3fn_x4
+FP4X4 = mybir.dt.float4_e2m1fn_x4
+ALU = mybir.AluOpType
+ACT = mybir.ActivationFunctionType
+
+P = 128
+PACK = 4
+GROUP = 4
+CHUNK = 128
+CHUNKS = J // CHUNK
+HALF = J // 2
+
+
+def tile_list_peak_gated_members_pl_kernel(
+    tc, xt, w_words, w_scales, xs_words, xs_scales, ws_words, ws_scales, offs, out_0, out_1, out_2
+):
+    nc = tc.nc
+    with ExitStack() as ctx:
+        sb = ctx.enter_context(tc.tile_pool(name="sb", bufs=1))
+        ps = ctx.enter_context(tc.psum_pool(name="ps", bufs=1))
+
+        x_rows = xt.rearrange("(z p t) c -> z t p c", z=2, t=PACK)
+        planes = [sb.tile([P, T], F32, name=f"plane{i}") for i in range(2 * PACK)]
+        nc.sync.dma_start(planes[0][:], x_rows[0, 0])
+        offsets = sb.tile([P, J // 16], U16, name="offsets")
+        nc.sync.dma_start(offsets[:], offs)
+
+        wsc_raw = sb.tile([P, 2, N], U8, name="wsc_raw")
+        wssc_raw = sb.tile([P, N], U8, name="wssc_raw")
+        xs_plane = sb.tile([P, J], U8, name="xs_plane", align_bytes=64)
+        nc.vector.memset(wsc_raw[:].bitcast(U32), 0)
+        nc.vector.memset(wssc_raw[:].bitcast(U32), 0)
+        nc.vector.memset(xs_plane[:].bitcast(U32), 0)
+
+        w_raw = sb.tile([P, 2, 2 * N], U8, name="w_raw")
+        nc.sync.dma_start(w_raw[:].bitcast(I32), w_words.rearrange("z p c -> p z c").bitcast(I32))
+        for q in range(4):
+            nc.sync.dma_start(
+                wsc_raw[32 * q : 32 * q + 4].bitcast(I32),
+                w_scales[:, 4 * q : 4 * q + 4, :].rearrange("z r c -> r z c").bitcast(I32),
+            )
+        nc.sync.dma_start(planes[1][:], x_rows[0, 1])
+        ws_raw = sb.tile([P, 2 * N], U8, name="ws_raw")
+        nc.sync.dma_start(ws_raw[:].bitcast(I32), ws_words[0].bitcast(I32))
+        for q in range(4):
+            nc.sync.dma_start(wssc_raw[32 * q : 32 * q + 4].bitcast(I32), ws_scales[0, 4 * q : 4 * q + 4, :].bitcast(I32))
+        nc.sync.dma_start(planes[2][:], x_rows[0, 2])
+        xs_codes = sb.tile([P, J], U32, name="xs_codes", align_bytes=64)
+        nc.sync.dma_start(xs_codes[:].bitcast(I32), xs_words[0].rearrange("p c r -> p (c r)").bitcast(I32))
+        for q in range(4):
+            nc.sync.dma_start(xs_plane[32 * q : 32 * q + 4].bitcast(I32), xs_scales[0, 4 * q : 4 * q + 4, :].bitcast(I32))
+        for i in range(3, 2 * PACK):
+            nc.sync.dma_start(planes[i][:], x_rows[i // PACK, i % PACK])
+
+        def deal(words, scale_bytes, name):
+            codes = sb.tile([P, PACK, P, 2], U8, name=name + "_codes", align_bytes=64)
+            nc.vector.tensor_copy(codes[:].rearrange("p t m b -> p m t b"), words.rearrange("p (m t b) -> p m t b", t=PACK, b=2))
+            return codes
+
+        def deal_scales(scale_bytes, name):
+            plane = sb.tile([P, PACK, P], U8, name=name + "_plane", align_bytes=64)
+            nc.vector.tensor_copy(plane[:].rearrange("p t m -> p m t"), scale_bytes.rearrange("p (m t) -> p m t", t=PACK))
+            return plane
+
+        w_codes = [deal(w_raw[:, z, :], None, f"w{z}") for z in range(2)]
+        ws_codes = deal(ws_raw[:], None, "ws")
+
+        def stationary(codes, plane, t):
+            return dict(lhsT=codes[:, t].rearrange("p m b -> p (m b)").bitcast(FP4X4), lhsT_scale=plane[:, t, :])
+
+        picked = sb.tile([P, PACK, J], F32, name="picked")
+        for t in range(PACK):
+            nc.vector.tensor_copy(picked[:, t, :], planes[t][:].indirect(offsets[:]))
+        w_planes = [deal_scales(wsc_raw[:, z, :], f"w{z}") for z in range(2)]
+        ws_plane = deal_scales(wssc_raw[:], "ws")
+        woven0 = sb.tile([P, J, PACK], BF16, name="woven0", align_bytes=64)
+        nc.scalar.copy(woven0[:].rearrange("p (c i) t -> p c t i", i=4), picked[:].rearrange("p t (c i) -> p c t i", i=4))
+        x_codes0 = sb.tile([P, J], U32, name="x_codes0", align_bytes=64)
+        x_plane0 = sb.tile([P, J], U8, name="x_plane0", align_bytes=64)
+        nc.vector.quantize_mx(x_codes0[:].bitcast(FP8X4), x_plane0[:], woven0[:].rearrange("p j t -> p (j t)"))
+
+        z_banks = [ps.tile([P, PACK, CHUNK], F32, name=f"z{c}") for c in range(CHUNKS)]
+        for c in range(CHUNKS):
+            cols = slice(c * CHUNK, (c + 1) * CHUNK)
+            for t in range(PACK):
+                nc.tensor.matmul_mx(
+                    z_banks[c][:, t, :], rhs=x_codes0[:, cols].bitcast(FP8X4), rhs_scale=x_plane0[:, cols],
+                    start=(t == 0), stop=False, **stationary(w_codes[0], w_planes[0], t),
+                )
+
+        q_banks = [ps.tile([P, PACK, CHUNK], F32, name=f"q{c}") for c in range(CHUNKS)]
+        half_q = {}
+        for c in range(CHUNKS):
+            cols = slice(c * CHUNK, (c + 1) * CHUNK)
+            for t in range(PACK):
+                nc.tensor.matmul_mx(
+                    q_banks[c][:, t, :], rhs=xs_codes[:, cols].bitcast(FP8X4), rhs_scale=xs_plane[:, cols],
+                    start=True, stop=True, **stationary(ws_codes, ws_plane, t),
+                )
+            if c < CHUNKS - 1:
+                half_q[c] = sb.tile([P, PACK, CHUNK], F32, name=f"half_q{c}")
+                nc.scalar.activation(half_q[c][:], q_banks[c][:], ACT.Copy, scale=0.5)
+
+        woven1 = [sb.tile([P, HALF, PACK], BF16, name=f"woven1_{h}", align_bytes=64) for h in range(2)]
+        for t in range(PACK):
+            for h in range(2):
+                cols = slice(h * HALF // 16, (h + 1) * HALF // 16)
+                nc.vector.tensor_copy(woven1[h][:, :, t], planes[PACK + t][:].indirect(offsets[:, cols]))
+                if t == PACK - 1:
+                    x_codes1 = sb.tile([P, HALF], U32, name=f"x_codes1_{h}", align_bytes=64)
+                    x_plane1 = sb.tile([P, HALF], U8, name=f"x_plane1_{h}", align_bytes=64)
+                    nc.vector.quantize_mx(x_codes1[:].bitcast(FP8X4), x_plane1[:], woven1[h][:].rearrange("p j t -> p (j t)"))
+                    for c in range(2 * h, 2 * h + 2):
+                        cols = slice((c % 2) * CHUNK, (c % 2 + 1) * CHUNK)
+                        for s in range(PACK):
+                            nc.tensor.matmul_mx(
+                                z_banks[c][:, s, :], rhs=x_codes1[:, cols].bitcast(FP8X4), rhs_scale=x_plane1[:, cols],
+                                start=False, stop=(s == PACK - 1), **stationary(w_codes[1], w_planes[1], s),
+                            )
+
+        y_codes = sb.tile([P, J], U32, name="y_codes", align_bytes=64)
+        y_plane = sb.tile([P, J], U8, name="y_plane", align_bytes=64)
+        y_rows = out_0.rearrange("(p t) j -> p t j", t=PACK)
+        words_out = out_1[0].rearrange("p c r -> p (c r)").bitcast(I32)
+        gap, gate, woven_y = {}, {}, {}
+
+        def peak_gap(c):
+            members = z_banks[c][:].rearrange("p t (b i) -> p (t b) i", i=GROUP)
+            peak = sb.tile([P, P], F32, name=f"peak{c}")
+            nc.vector.tensor_reduce(peak[:], members, mybir.AxisListType.X, ALU.max)
+            gap[c] = sb.tile([P, P, GROUP], F32, name=f"gap{c}")
+            nc.vector.tensor_tensor(gap[c][:], members, peak[:].unsqueeze(2).to_broadcast([P, P, GROUP]), ALU.subtract)
+            gate[c] = sb.tile([P, PACK, CHUNK], F32, name=f"gate{c}")
+            nc.scalar.activation(gate[c][:].rearrange("p t j -> p (t j)"), gap[c][:].rearrange("p g i -> p (g i)"), ACT.Exp)
+
+        def combine(c):
+            cols = slice(c * CHUNK, (c + 1) * CHUNK)
+            gated = sb.tile([P, PACK, CHUNK], F32, name=f"gated{c}")
+            nc.vector.tensor_tensor(gated[:], z_banks[c][:], gate[c][:], ALU.mult)
+            y = sb.tile([P, PACK, CHUNK], F32, name=f"y{c}")
+            nc.gpsimd.tensor_tensor(y[:], gated[:], half_q[c][:], ALU.add)
+            nc.sync.dma_start(y_rows[:, :, cols], y[:])
+            woven_y[c] = sb.tile([P, CHUNK, PACK], BF16, name=f"woven_y{c}", align_bytes=64)
+            nc.scalar.copy(woven_y[c][:].rearrange("p (c i) t -> p c t i", i=4), y[:].rearrange("p t (c i) -> p c t i", i=4))
+
+        def requantise(c):
+            cols = slice(c * CHUNK, (c + 1) * CHUNK)
+            nc.vector.quantize_mx(y_codes[:, cols].bitcast(FP8X4), y_plane[:, cols], woven_y[c][:].rearrange("p j t -> p (j t)"))
+            nc.sync.dma_start(words_out[:, cols], y_codes[:, cols].bitcast(I32))
+
+        def finish(c):
+            halves = [slice(0, CHUNK // 2), slice(CHUNK // 2, CHUNK)]
+            cols = slice(c * CHUNK, (c + 1) * CHUNK)
+            gated = [sb.tile([P, PACK, CHUNK // 2], F32, name=f"gated{c}_{h}") for h in range(2)]
+            woven = [sb.tile([P, CHUNK // 2, PACK], BF16, name=f"woven_y{c}_{h}", align_bytes=64) for h in range(2)]
+            y = sb.tile([P, PACK, CHUNK], F32, name=f"y{c}")
+            for h in range(2):
+                nc.vector.tensor_tensor(gated[h][:], z_banks[c][:, :, halves[h]], gate[c][:, :, halves[h]], ALU.mult)
+            for h in range(2):
+                nc.vector.scalar_tensor_tensor(y[:, :, halves[h]], q_banks[c][:, :, halves[h]], 0.5, gated[h][:], ALU.mult, ALU.add)
+            nc.sync.dma_start(y_rows[:, :, cols], y[:])
+            for h in range(2):
+                nc.vector.tensor_copy(woven[h][:].rearrange("p (c i) t -> p c t i", i=4), y[:, :, halves[h]].rearrange("p t (c i) -> p c t i", i=4))
+            requantise(c - 2)
+            for h in range(2):
+                part = slice(c * CHUNK + halves[h].start, c * CHUNK + halves[h].stop)
+                nc.vector.quantize_mx(y_codes[:, part].bitcast(FP8X4), y_plane[:, part], woven[h][:].rearrange("p j t -> p (j t)"))
+            nc.scalar.dma_start(words_out[:, cols], y_codes[:, cols].bitcast(I32))
+            requantise(c - 1)
+
+        peak_gap(0)
+        peak_gap(1)
+        peak_gap(2)
+        combine(0)
+        peak_gap(3)
+        combine(1)
+        combine(2)
+        requantise(0)
+        finish(3)
+        for q in range(4):
+            queue = nc.sync if q % 2 == 0 else nc.scalar
+            queue.dma_start(out_2[0, 4 * q : 4 * q + 4, :].bitcast(I32), y_plane[32 * q : 32 * q + 4, :].bitcast(I32))

@@ -33,7 +33,7 @@ def tile_list_peak_gated_members_pl_kernel(
         ps = ctx.enter_context(tc.psum_pool(name="ps", bufs=1))
 
         x_rows = xt.rearrange("(z p t) c -> z t p c", z=2, t=PACK)
-        planes = [sb.tile([P, T], F32, name=f"plane{i}") for i in range(2 * PACK)]
+        planes = [sb.tile([P, T], F32, name=f"plane{i}", align_bytes=64) for i in range(2 * PACK)]
         nc.sync.dma_start(planes[0][:], x_rows[0, 0])
         offsets = sb.tile([P, J // 16], U16, name="offsets")
         nc.sync.dma_start(offsets[:], offs)
@@ -45,34 +45,35 @@ def tile_list_peak_gated_members_pl_kernel(
         nc.vector.memset(wssc_raw[:].bitcast(U32), 0)
         nc.vector.memset(xs_plane[:].bitcast(U32), 0)
 
-        w_raw = sb.tile([P, 2, 2 * N], U8, name="w_raw")
-        nc.sync.dma_start(w_raw[:].bitcast(I32), w_words.rearrange("z p c -> p z c").bitcast(I32))
         for q in range(4):
-            nc.sync.dma_start(
+            nc.gpsimd.dma_start(
                 wsc_raw[32 * q : 32 * q + 4].bitcast(I32),
                 w_scales[:, 4 * q : 4 * q + 4, :].rearrange("z r c -> r z c").bitcast(I32),
             )
+        for q in range(4):
+            nc.gpsimd.dma_start(wssc_raw[32 * q : 32 * q + 4].bitcast(I32), ws_scales[0, 4 * q : 4 * q + 4, :].bitcast(I32))
+        for q in range(4):
+            nc.gpsimd.dma_start(xs_plane[32 * q : 32 * q + 4].bitcast(I32), xs_scales[0, 4 * q : 4 * q + 4, :].bitcast(I32))
+
+        w_raw = sb.tile([P, 2, 2 * N], U8, name="w_raw")
+        nc.sync.dma_start(w_raw[:].bitcast(I32), w_words.rearrange("z p c -> p z c").bitcast(I32))
         nc.sync.dma_start(planes[1][:], x_rows[0, 1])
         ws_raw = sb.tile([P, 2 * N], U8, name="ws_raw")
         nc.sync.dma_start(ws_raw[:].bitcast(I32), ws_words[0].bitcast(I32))
-        for q in range(4):
-            nc.sync.dma_start(wssc_raw[32 * q : 32 * q + 4].bitcast(I32), ws_scales[0, 4 * q : 4 * q + 4, :].bitcast(I32))
         nc.sync.dma_start(planes[2][:], x_rows[0, 2])
         xs_codes = sb.tile([P, J], U32, name="xs_codes", align_bytes=64)
         nc.sync.dma_start(xs_codes[:].bitcast(I32), xs_words[0].rearrange("p c r -> p (c r)").bitcast(I32))
-        for q in range(4):
-            nc.sync.dma_start(xs_plane[32 * q : 32 * q + 4].bitcast(I32), xs_scales[0, 4 * q : 4 * q + 4, :].bitcast(I32))
         for i in range(3, 2 * PACK):
             nc.sync.dma_start(planes[i][:], x_rows[i // PACK, i % PACK])
 
         def deal(words, scale_bytes, name):
             codes = sb.tile([P, PACK, P, 2], U8, name=name + "_codes", align_bytes=64)
-            nc.vector.tensor_copy(codes[:].rearrange("p t m b -> p m t b"), words.rearrange("p (m t b) -> p m t b", t=PACK, b=2))
+            nc.vector.tensor_copy(codes[:], words.rearrange("p (m t b) -> p t m b", t=PACK, b=2))
             return codes
 
-        def deal_scales(scale_bytes, name):
-            plane = sb.tile([P, PACK, P], U8, name=name + "_plane", align_bytes=64)
-            nc.vector.tensor_copy(plane[:].rearrange("p t m -> p m t"), scale_bytes.rearrange("p (m t) -> p m t", t=PACK))
+        def deal_scales(scale_bytes, name, slot):
+            plane = sb.tile([P, PACK, P], U8, name=name + "_plane", tag=f"plane{slot}", align_bytes=64)
+            nc.vector.tensor_copy(plane[:], scale_bytes.rearrange("p (m t) -> p t m", t=PACK))
             return plane
 
         w_codes = [deal(w_raw[:, z, :], None, f"w{z}") for z in range(2)]
@@ -84,8 +85,8 @@ def tile_list_peak_gated_members_pl_kernel(
         picked = sb.tile([P, PACK, J], F32, name="picked")
         for t in range(PACK):
             nc.vector.tensor_copy(picked[:, t, :], planes[t][:].indirect(offsets[:]))
-        w_planes = [deal_scales(wsc_raw[:, z, :], f"w{z}") for z in range(2)]
-        ws_plane = deal_scales(wssc_raw[:], "ws")
+        w_planes = [deal_scales(wsc_raw[:, z, :], f"w{z}", 1 + z) for z in range(2)]
+        ws_plane = deal_scales(wssc_raw[:], "ws", 3)
         woven0 = sb.tile([P, J, PACK], BF16, name="woven0", align_bytes=64)
         nc.scalar.copy(woven0[:].rearrange("p (c i) t -> p c t i", i=4), picked[:].rearrange("p t (c i) -> p c t i", i=4))
         x_codes0 = sb.tile([P, J], U32, name="x_codes0", align_bytes=64)
@@ -110,7 +111,7 @@ def tile_list_peak_gated_members_pl_kernel(
                     q_banks[c][:, t, :], rhs=xs_codes[:, cols].bitcast(FP8X4), rhs_scale=xs_plane[:, cols],
                     start=True, stop=True, **stationary(ws_codes, ws_plane, t),
                 )
-            if c < CHUNKS - 1:
+            if c < 2:
                 half_q[c] = sb.tile([P, PACK, CHUNK], F32, name=f"half_q{c}")
                 nc.scalar.activation(half_q[c][:], q_banks[c][:], ACT.Copy, scale=0.5)
 
@@ -135,37 +136,49 @@ def tile_list_peak_gated_members_pl_kernel(
         y_plane = sb.tile([P, J], U8, name="y_plane", align_bytes=64)
         y_rows = out_0.rearrange("(p t) j -> p t j", t=PACK)
         words_out = out_1[0].rearrange("p c r -> p (c r)").bitcast(I32)
-        gap, gate, woven_y = {}, {}, {}
+        gap, gate = {}, {}
 
         def peak_gap(c):
             members = z_banks[c][:].rearrange("p t (b i) -> p (t b) i", i=GROUP)
+            subtractor = nc.vector
             peak = sb.tile([P, P], F32, name=f"peak{c}")
+            if c % 2 == 0:
+                z_copy = sb.tile([P, P, GROUP], F32, name=f"z_copy{c}")
+                nc.scalar.copy(z_copy[:], members)
             nc.vector.tensor_reduce(peak[:], members, mybir.AxisListType.X, ALU.max)
+            if c % 2 == 0:
+                members, subtractor = z_copy[:], nc.gpsimd
             gap[c] = sb.tile([P, P, GROUP], F32, name=f"gap{c}")
-            nc.vector.tensor_tensor(gap[c][:], members, peak[:].unsqueeze(2).to_broadcast([P, P, GROUP]), ALU.subtract)
+            subtractor.tensor_tensor(gap[c][:], members, peak[:].unsqueeze(2).to_broadcast([P, P, GROUP]), ALU.subtract)
             gate[c] = sb.tile([P, PACK, CHUNK], F32, name=f"gate{c}")
             nc.scalar.activation(gate[c][:].rearrange("p t j -> p (t j)"), gap[c][:].rearrange("p g i -> p (g i)"), ACT.Exp)
+
+        woven_y = [sb.tile([P, HALF, PACK], BF16, name=f"woven_y{h}", align_bytes=64) for h in range(2)]
+
+        def weave(copy, out, y):
+            copy(out.rearrange("p (c i) t -> p c t i", i=4), y.rearrange("p t (c i) -> p c t i", i=4))
 
         def combine(c):
             cols = slice(c * CHUNK, (c + 1) * CHUNK)
             gated = sb.tile([P, PACK, CHUNK], F32, name=f"gated{c}")
             nc.vector.tensor_tensor(gated[:], z_banks[c][:], gate[c][:], ALU.mult)
             y = sb.tile([P, PACK, CHUNK], F32, name=f"y{c}")
-            nc.gpsimd.tensor_tensor(y[:], gated[:], half_q[c][:], ALU.add)
+            if c in half_q:
+                nc.gpsimd.tensor_tensor(y[:], gated[:], half_q[c][:], ALU.add)
+            else:
+                nc.vector.scalar_tensor_tensor(y[:], q_banks[c][:], 0.5, gated[:], ALU.mult, ALU.add)
             nc.sync.dma_start(y_rows[:, :, cols], y[:])
-            woven_y[c] = sb.tile([P, CHUNK, PACK], BF16, name=f"woven_y{c}", align_bytes=64)
-            nc.scalar.copy(woven_y[c][:].rearrange("p (c i) t -> p c t i", i=4), y[:].rearrange("p t (c i) -> p c t i", i=4))
+            weave(nc.scalar.copy, woven_y[c // 2][:, (c % 2) * CHUNK : (c % 2 + 1) * CHUNK, :], y[:])
 
-        def requantise(c):
-            cols = slice(c * CHUNK, (c + 1) * CHUNK)
-            nc.vector.quantize_mx(y_codes[:, cols].bitcast(FP8X4), y_plane[:, cols], woven_y[c][:].rearrange("p j t -> p (j t)"))
-            nc.sync.dma_start(words_out[:, cols], y_codes[:, cols].bitcast(I32))
+        def requantise(first, last, woven):
+            cols = slice(first, last)
+            nc.vector.quantize_mx(y_codes[:, cols].bitcast(FP8X4), y_plane[:, cols], woven.rearrange("p j t -> p (j t)"))
 
         def finish(c):
             halves = [slice(0, CHUNK // 2), slice(CHUNK // 2, CHUNK)]
             cols = slice(c * CHUNK, (c + 1) * CHUNK)
             gated = [sb.tile([P, PACK, CHUNK // 2], F32, name=f"gated{c}_{h}") for h in range(2)]
-            woven = [sb.tile([P, CHUNK // 2, PACK], BF16, name=f"woven_y{c}_{h}", align_bytes=64) for h in range(2)]
+            woven = [sb.tile([P, CHUNK // 2, PACK], BF16, name=f"woven_last{h}", align_bytes=64) for h in range(2)]
             y = sb.tile([P, PACK, CHUNK], F32, name=f"y{c}")
             for h in range(2):
                 nc.vector.tensor_tensor(gated[h][:], z_banks[c][:, :, halves[h]], gate[c][:, :, halves[h]], ALU.mult)
@@ -173,23 +186,22 @@ def tile_list_peak_gated_members_pl_kernel(
                 nc.vector.scalar_tensor_tensor(y[:, :, halves[h]], q_banks[c][:, :, halves[h]], 0.5, gated[h][:], ALU.mult, ALU.add)
             nc.sync.dma_start(y_rows[:, :, cols], y[:])
             for h in range(2):
-                nc.vector.tensor_copy(woven[h][:].rearrange("p (c i) t -> p c t i", i=4), y[:, :, halves[h]].rearrange("p t (c i) -> p c t i", i=4))
-            requantise(c - 2)
+                weave(nc.vector.tensor_copy, woven[h][:], y[:, :, halves[h]])
+            requantise(0, HALF, woven_y[0][:])
+            nc.scalar.dma_start(words_out[:, :HALF], y_codes[:, :HALF].bitcast(I32))
+            requantise(HALF, HALF + CHUNK, woven_y[1][:, :CHUNK, :])
             for h in range(2):
-                part = slice(c * CHUNK + halves[h].start, c * CHUNK + halves[h].stop)
-                nc.vector.quantize_mx(y_codes[:, part].bitcast(FP8X4), y_plane[:, part], woven[h][:].rearrange("p j t -> p (j t)"))
-            nc.scalar.dma_start(words_out[:, cols], y_codes[:, cols].bitcast(I32))
-            requantise(c - 1)
+                requantise(c * CHUNK + halves[h].start, c * CHUNK + halves[h].stop, woven[h][:])
+            nc.sync.dma_start(words_out[:, HALF:], y_codes[:, HALF:].bitcast(I32))
 
         peak_gap(0)
         peak_gap(1)
         peak_gap(2)
-        combine(0)
         peak_gap(3)
+        combine(0)
         combine(1)
         combine(2)
-        requantise(0)
         finish(3)
         for q in range(4):
-            queue = nc.sync if q % 2 == 0 else nc.scalar
+            queue = nc.scalar if q % 2 == 0 else nc.sync
             queue.dma_start(out_2[0, 4 * q : 4 * q + 4, :].bitcast(I32), y_plane[32 * q : 32 * q + 4, :].bitcast(I32))

@@ -34,6 +34,10 @@ def tile_list_peak_gated_members_pl_kernel(
 
         x_rows = xt.rearrange("(z p t) c -> z t p c", z=2, t=PACK)
         planes = [sb.tile([P, T], F32, name=f"plane{i}", align_bytes=64) for i in range(2 * PACK)]
+        w_raw = sb.tile([P, 2, 2 * N], U8, name="w_raw")
+        nc.sync.dma_start(w_raw[:].bitcast(I32), w_words.rearrange("z p c -> p z c").bitcast(I32))
+        ws_raw = sb.tile([P, 2 * N], U8, name="ws_raw")
+        nc.sync.dma_start(ws_raw[:].bitcast(I32), ws_words[0].bitcast(I32))
         nc.sync.dma_start(planes[0][:], x_rows[0, 0])
         offsets = sb.tile([P, J // 16], U16, name="offsets")
         nc.sync.dma_start(offsets[:], offs)
@@ -55,11 +59,7 @@ def tile_list_peak_gated_members_pl_kernel(
         for q in range(4):
             nc.gpsimd.dma_start(xs_plane[32 * q : 32 * q + 4].bitcast(I32), xs_scales[0, 4 * q : 4 * q + 4, :].bitcast(I32))
 
-        w_raw = sb.tile([P, 2, 2 * N], U8, name="w_raw")
-        nc.sync.dma_start(w_raw[:].bitcast(I32), w_words.rearrange("z p c -> p z c").bitcast(I32))
         nc.sync.dma_start(planes[1][:], x_rows[0, 1])
-        ws_raw = sb.tile([P, 2 * N], U8, name="ws_raw")
-        nc.sync.dma_start(ws_raw[:].bitcast(I32), ws_words[0].bitcast(I32))
         nc.sync.dma_start(planes[2][:], x_rows[0, 2])
         xs_codes = sb.tile([P, J], U32, name="xs_codes", align_bytes=64)
         nc.sync.dma_start(xs_codes[:].bitcast(I32), xs_words[0].rearrange("p c r -> p (c r)").bitcast(I32))
@@ -67,8 +67,8 @@ def tile_list_peak_gated_members_pl_kernel(
             nc.sync.dma_start(planes[i][:], x_rows[i // PACK, i % PACK])
 
         def deal(words, scale_bytes, name):
-            codes = sb.tile([P, PACK, P, 2], U8, name=name + "_codes", align_bytes=64)
-            nc.vector.tensor_copy(codes[:], words.rearrange("p (m t b) -> p t m b", t=PACK, b=2))
+            codes = sb.tile([P, PACK, P], U16, name=name + "_codes", align_bytes=64)
+            nc.vector.tensor_copy(codes[:], words.bitcast(U16).rearrange("p (m t) -> p t m", t=PACK))
             return codes
 
         def deal_scales(scale_bytes, name, slot):
@@ -80,7 +80,7 @@ def tile_list_peak_gated_members_pl_kernel(
         ws_codes = deal(ws_raw[:], None, "ws")
 
         def stationary(codes, plane, t):
-            return dict(lhsT=codes[:, t].rearrange("p m b -> p (m b)").bitcast(FP4X4), lhsT_scale=plane[:, t, :])
+            return dict(lhsT=codes[:, t, :].bitcast(FP4X4), lhsT_scale=plane[:, t, :])
 
         picked = sb.tile([P, PACK, J], F32, name="picked")
         for t in range(PACK):
@@ -116,7 +116,12 @@ def tile_list_peak_gated_members_pl_kernel(
                 nc.scalar.activation(half_q[c][:], q_banks[c][:], ACT.Copy, scale=0.5)
 
         woven1 = [sb.tile([P, HALF, PACK], BF16, name=f"woven1_{h}", align_bytes=64) for h in range(2)]
-        for t in range(PACK):
+        picked1 = sb.tile([P, 2, J], F32, name="picked1")
+        for t in range(2):
+            nc.vector.tensor_copy(picked1[:, t, :], planes[PACK + t][:].indirect(offsets[:]))
+        for h in range(2):
+            nc.scalar.copy(woven1[h][:, :, 0:2], picked1[:, :, h * HALF : (h + 1) * HALF].rearrange("p t j -> p j t"))
+        for t in range(2, PACK):
             for h in range(2):
                 cols = slice(h * HALF // 16, (h + 1) * HALF // 16)
                 nc.vector.tensor_copy(woven1[h][:, :, t], planes[PACK + t][:].indirect(offsets[:, cols]))

from contextlib import ExitStack

import concourse.mybir as mybir

K, T, J, N = 1024, 2048, 512, 512
FLOPS = 2 * (K + 512) * N * J

F32 = mybir.dt.float32
BF16 = mybir.dt.bfloat16
I32 = mybir.dt.int32
U32 = mybir.dt.uint32
U16 = mybir.dt.uint16
U8 = mybir.dt.uint8
FP8X4 = mybir.dt.float8_e4m3fn_x4
FP4X4 = mybir.dt.float4_e2m1fn_x4
ALU = mybir.AluOpType
ACT = mybir.ActivationFunctionType

P = 128
PACK = 4
GROUP = 4
CHUNK = 128
CHUNKS = J // CHUNK
HALF = J // 2


def tile_list_peak_gated_members_pl_kernel(
    tc, xt, w_words, w_scales, xs_words, xs_scales, ws_words, ws_scales, offs, out_0, out_1, out_2
):
    nc = tc.nc
    with ExitStack() as ctx:
        sb = ctx.enter_context(tc.tile_pool(name="sb", bufs=1))
        ps = ctx.enter_context(tc.psum_pool(name="ps", bufs=1))

        x_rows = xt.rearrange("(z p t) c -> z t p c", z=2, t=PACK)
        planes = [sb.tile([P, T], F32, name=f"plane{i}", align_bytes=64) for i in range(2 * PACK)]
        w_raw = sb.tile([P, 2, 2 * N], U8, name="w_raw")
        nc.sync.dma_start(w_raw[:].bitcast(I32), w_words.rearrange("z p c -> p z c").bitcast(I32))
        ws_raw = sb.tile([P, 2 * N], U8, name="ws_raw")
        nc.sync.dma_start(ws_raw[:].bitcast(I32), ws_words[0].bitcast(I32))
        nc.sync.dma_start(planes[0][:], x_rows[0, 0])
        offsets = sb.tile([P, J // 16], U16, name="offsets")
        nc.sync.dma_start(offsets[:], offs)

        wsc_raw = sb.tile([P, 2, N], U8, name="wsc_raw")
        wssc_raw = sb.tile([P, N], U8, name="wssc_raw")
        xs_plane = sb.tile([P, J], U8, name="xs_plane", align_bytes=64)
        nc.vector.memset(wsc_raw[:].bitcast(U32), 0)
        nc.vector.memset(wssc_raw[:].bitcast(U32), 0)
        nc.vector.memset(xs_plane[:].bitcast(U32), 0)

        for q in range(4):
            nc.gpsimd.dma_start(
                wsc_raw[32 * q : 32 * q + 4].bitcast(I32),
                w_scales[:, 4 * q : 4 * q + 4, :].rearrange("z r c -> r z c").bitcast(I32),
            )
        for q in range(4):
            nc.gpsimd.dma_start(wssc_raw[32 * q : 32 * q + 4].bitcast(I32), ws_scales[0, 4 * q : 4 * q + 4, :].bitcast(I32))
        for q in range(4):
            nc.gpsimd.dma_start(xs_plane[32 * q : 32 * q + 4].bitcast(I32), xs_scales[0, 4 * q : 4 * q + 4, :].bitcast(I32))

        nc.sync.dma_start(planes[1][:], x_rows[0, 1])
        nc.sync.dma_start(planes[2][:], x_rows[0, 2])
        xs_codes = sb.tile([P, J], U32, name="xs_codes", align_bytes=64)
        nc.sync.dma_start(xs_codes[:].bitcast(I32), xs_words[0].rearrange("p c r -> p (c r)").bitcast(I32))
        for i in range(3, 2 * PACK):
            nc.sync.dma_start(planes[i][:], x_rows[i // PACK, i % PACK])

        def deal(words, scale_bytes, name):
            codes = sb.tile([P, PACK, P], U16, name=name + "_codes", align_bytes=64)
            nc.vector.tensor_copy(codes[:], words.bitcast(U16).rearrange("p (m t) -> p t m", t=PACK))
            return codes

        def deal_scales(scale_bytes, name, slot):
            plane = sb.tile([P, PACK, P], U8, name=name + "_plane", tag=f"plane{slot}", align_bytes=64)
            nc.vector.tensor_copy(plane[:], scale_bytes.rearrange("p (m t) -> p t m", t=PACK))
            return plane

        w_codes = [deal(w_raw[:, z, :], None, f"w{z}") for z in range(2)]
        ws_codes = deal(ws_raw[:], None, "ws")

        def stationary(codes, plane, t):
            return dict(lhsT=codes[:, t, :].bitcast(FP4X4), lhsT_scale=plane[:, t, :])

        picked = sb.tile([P, PACK, J], F32, name="picked")
        for t in range(PACK):
            nc.vector.tensor_copy(picked[:, t, :], planes[t][:].indirect(offsets[:]))
        w_planes = [deal_scales(wsc_raw[:, z, :], f"w{z}", 1 + z) for z in range(2)]
        ws_plane = deal_scales(wssc_raw[:], "ws", 3)
        woven0 = sb.tile([P, J, PACK], BF16, name="woven0", align_bytes=64)
        nc.scalar.copy(woven0[:].rearrange("p (c i) t -> p c t i", i=4), picked[:].rearrange("p t (c i) -> p c t i", i=4))
        x_codes0 = sb.tile([P, J], U32, name="x_codes0", align_bytes=64)
        x_plane0 = sb.tile([P, J], U8, name="x_plane0", align_bytes=64)
        nc.vector.quantize_mx(x_codes0[:].bitcast(FP8X4), x_plane0[:], woven0[:].rearrange("p j t -> p (j t)"))

        z_banks = [ps.tile([P, PACK, CHUNK], F32, name=f"z{c}") for c in range(CHUNKS)]
        for c in range(CHUNKS):
            cols = slice(c * CHUNK, (c + 1) * CHUNK)
            for t in range(PACK):
                nc.tensor.matmul_mx(
                    z_banks[c][:, t, :], rhs=x_codes0[:, cols].bitcast(FP8X4), rhs_scale=x_plane0[:, cols],
                    start=(t == 0), stop=False, **stationary(w_codes[0], w_planes[0], t),
                )

        q_banks = [ps.tile([P, PACK, CHUNK], F32, name=f"q{c}") for c in range(CHUNKS)]
        half_q = {}
        for c in range(CHUNKS):
            cols = slice(c * CHUNK, (c + 1) * CHUNK)
            for t in range(PACK):
                nc.tensor.matmul_mx(
                    q_banks[c][:, t, :], rhs=xs_codes[:, cols].bitcast(FP8X4), rhs_scale=xs_plane[:, cols],
                    start=True, stop=True, **stationary(ws_codes, ws_plane, t),
                )
            if c < 2:
                half_q[c] = sb.tile([P, PACK, CHUNK], F32, name=f"half_q{c}")
                nc.scalar.activation(half_q[c][:], q_banks[c][:], ACT.Copy, scale=0.5)

        woven1 = [sb.tile([P, HALF, PACK], BF16, name=f"woven1_{h}", align_bytes=64) for h in range(2)]
        picked1 = sb.tile([P, 2, J], F32, name="picked1")
        for t in range(2):
            nc.vector.tensor_copy(picked1[:, t, :], planes[PACK + t][:].indirect(offsets[:]))
        for h in range(2):
            nc.scalar.copy(woven1[h][:, :, 0:2], picked1[:, :, h * HALF : (h + 1) * HALF].rearrange("p t j -> p j t"))
        for t in range(2, PACK):
            for h in range(2):
                cols = slice(h * HALF // 16, (h + 1) * HALF // 16)
                nc.vector.tensor_copy(woven1[h][:, :, t], planes[PACK + t][:].indirect(offsets[:, cols]))
                if t == PACK - 1:
                    x_codes1 = sb.tile([P, HALF], U32, name=f"x_codes1_{h}", align_bytes=64)
                    x_plane1 = sb.tile([P, HALF], U8, name=f"x_plane1_{h}", align_bytes=64)
                    nc.vector.quantize_mx(x_codes1[:].bitcast(FP8X4), x_plane1[:], woven1[h][:].rearrange("p j t -> p (j t)"))
                    for c in range(2 * h, 2 * h + 2):
                        cols = slice((c % 2) * CHUNK, (c % 2 + 1) * CHUNK)
                        for s in range(PACK):
                            nc.tensor.matmul_mx(
                                z_banks[c][:, s, :], rhs=x_codes1[:, cols].bitcast(FP8X4), rhs_scale=x_plane1[:, cols],
                                start=False, stop=(s == PACK - 1), **stationary(w_codes[1], w_planes[1], s),
                            )

        y_codes = sb.tile([P, J], U32, name="y_codes", align_bytes=64)
        y_plane = sb.tile([P, J], U8, name="y_plane", align_bytes=64)
        y_rows = out_0.rearrange("(p t) j -> p t j", t=PACK)
        words_out = out_1[0].rearrange("p c r -> p (c r)").bitcast(I32)
        gap, gate = {}, {}

        def peak_gap(c):
            members = z_banks[c][:].rearrange("p t (b i) -> p (t b) i", i=GROUP)
            subtractor = nc.vector
            peak = sb.tile([P, P], F32, name=f"peak{c}")
            if c % 2 == 0:
                z_copy = sb.tile([P, P, GROUP], F32, name=f"z_copy{c}")
                nc.scalar.copy(z_copy[:], members)
            nc.vector.tensor_reduce(peak[:], members, mybir.AxisListType.X, ALU.max)
            if c % 2 == 0:
                members, subtractor = z_copy[:], nc.gpsimd
            gap[c] = sb.tile([P, P, GROUP], F32, name=f"gap{c}")
            subtractor.tensor_tensor(gap[c][:], members, peak[:].unsqueeze(2).to_broadcast([P, P, GROUP]), ALU.subtract)
            gate[c] = sb.tile([P, PACK, CHUNK], F32, name=f"gate{c}")
            nc.scalar.activation(gate[c][:].rearrange("p t j -> p (t j)"), gap[c][:].rearrange("p g i -> p (g i)"), ACT.Exp)

        woven_y = [sb.tile([P, HALF, PACK], BF16, name=f"woven_y{h}", align_bytes=64) for h in range(2)]

        def weave(copy, out, y):
            copy(out.rearrange("p (c i) t -> p c t i", i=4), y.rearrange("p t (c i) -> p c t i", i=4))

        def combine(c):
            cols = slice(c * CHUNK, (c + 1) * CHUNK)
            gated = sb.tile([P, PACK, CHUNK], F32, name=f"gated{c}")
            nc.vector.tensor_tensor(gated[:], z_banks[c][:], gate[c][:], ALU.mult)
            y = sb.tile([P, PACK, CHUNK], F32, name=f"y{c}")
            if c in half_q:
                nc.gpsimd.tensor_tensor(y[:], gated[:], half_q[c][:], ALU.add)
            else:
                nc.vector.scalar_tensor_tensor(y[:], q_banks[c][:], 0.5, gated[:], ALU.mult, ALU.add)
            nc.sync.dma_start(y_rows[:, :, cols], y[:])
            weave(nc.scalar.copy, woven_y[c // 2][:, (c % 2) * CHUNK : (c % 2 + 1) * CHUNK, :], y[:])

        def requantise(first, last, woven):
            cols = slice(first, last)
            nc.vector.quantize_mx(y_codes[:, cols].bitcast(FP8X4), y_plane[:, cols], woven.rearrange("p j t -> p (j t)"))

        def finish(c):
            halves = [slice(0, CHUNK // 2), slice(CHUNK // 2, CHUNK)]
            cols = slice(c * CHUNK, (c + 1) * CHUNK)
            gated = [sb.tile([P, PACK, CHUNK // 2], F32, name=f"gated{c}_{h}") for h in range(2)]
            woven = [sb.tile([P, CHUNK // 2, PACK], BF16, name=f"woven_last{h}", align_bytes=64) for h in range(2)]
            y = sb.tile([P, PACK, CHUNK], F32, name=f"y{c}")
            for h in range(2):
                nc.vector.tensor_tensor(gated[h][:], z_banks[c][:, :, halves[h]], gate[c][:, :, halves[h]], ALU.mult)
            for h in range(2):
                nc.vector.scalar_tensor_tensor(y[:, :, halves[h]], q_banks[c][:, :, halves[h]], 0.5, gated[h][:], ALU.mult, ALU.add)
            nc.sync.dma_start(y_rows[:, :, cols], y[:])
            for h in range(2):
                weave(nc.vector.tensor_copy, woven[h][:], y[:, :, halves[h]])
            requantise(0, HALF, woven_y[0][:])
            nc.scalar.dma_start(words_out[:, :HALF], y_codes[:, :HALF].bitcast(I32))
            requantise(HALF, HALF + CHUNK, woven_y[1][:, :CHUNK, :])
            for h in range(2):
                requantise(c * CHUNK + halves[h].start, c * CHUNK + halves[h].stop, woven[h][:])
            nc.sync.dma_start(words_out[:, HALF:], y_codes[:, HALF:].bitcast(I32))

        peak_gap(0)
        peak_gap(1)
        peak_gap(2)
        peak_gap(3)
        combine(0)
        combine(1)
        combine(2)
        finish(3)
        for q in range(4):
            queue = nc.scalar if q % 2 == 0 else nc.sync
            queue.dma_start(out_2[0, 4 * q : 4 * q + 4, :].bitcast(I32), y_plane[32 * q : 32 * q + 4, :].bitcast(I32))
